import numpy as np
import ml_dtypes


def mxq(x, axis, fmt="e4m3"):
    dtype, down = {"e4m3": (ml_dtypes.float8_e4m3fn, 7), "e5m2": (ml_dtypes.float8_e5m2, 14)}[fmt]
    v = np.moveaxis(np.asarray(x, np.float32).astype(ml_dtypes.bfloat16).astype(np.float64), axis, -1)
    blocks = v.reshape(v.shape[:-1] + (-1, 32))
    amax = np.abs(blocks).max(-1, keepdims=True)
    byte = np.maximum(np.where(amax > 0, np.frexp(amax)[1] - 1 + 127, 0) - down, 1)
    scale = np.exp2(byte - 127.0)
    codes = (blocks / scale).astype(np.float32).astype(dtype).astype(np.float64)
    return np.moveaxis((codes * scale).reshape(v.shape), -1, axis)


WIDE = False


def mx_kscale(k):
    if not WIDE:
        return np.ones(k)
    levels = np.array([10, -10, 5, -5, 0])
    if k % 512:
        return np.exp2(np.random.permutation(np.resize(levels, k // 32))).repeat(32)
    a = np.empty((k // 512, 16))
    for p in range(k // 512):
        a[p, :8] = np.random.permutation(np.resize(levels, 8))
        for g in range(8):
            far = levels[np.abs(levels - a[p, g]) >= 10]
            a[p, g + 8] = far[np.random.randint(len(far))]
    return np.exp2(a.ravel()).repeat(32)


def f64(x):
    return np.asarray(x).astype(np.float64)


def striped8(idx):
    return np.asarray(idx).reshape(8, -1, 16).transpose(0, 2, 1).reshape(128, -1).astype(np.uint16)


def unstriped8(offs):
    return offs.reshape(8, 16, -1).transpose(0, 2, 1).reshape(8, -1).astype(np.int64)


def pick8(x, idx, run):
    r = np.arange(len(x))
    return x[r[:, None], idx[r % (8 * run) // run]]


E2M1 = np.array([0.0, 0.5, 1.0, 1.5, 2.0, 3.0, 4.0, 6.0, -0.0, -0.5, -1.0, -1.5, -2.0, -3.0, -4.0, -6.0])


def pack_weight(w, fmt):
    k, n = w.shape
    w = f64(np.asarray(w, np.float32).astype(ml_dtypes.bfloat16)).reshape(k // 32, 32, n)
    amax = np.abs(w).max(1)
    if fmt == "e4m3":
        byte = np.frexp(amax)[1] - 1 + 127 - 7
    else:
        mant, ex = np.frexp(amax / 6.0)
        byte = np.where(mant > 0.5, ex, ex - 1) + 127
    byte = np.clip(np.where(amax > 0, byte, 1), 1, 254)
    scaled = (w * np.exp2(127.0 - byte)[:, None, :]).reshape(k, n).astype(np.float32)
    by_word = np.ascontiguousarray(scaled.reshape(k // 512, 128, 4, n).transpose(0, 1, 3, 2))
    if fmt == "e4m3":
        words = by_word.astype(ml_dtypes.float8_e4m3fn).view(np.uint8)
    else:
        c = by_word.astype(ml_dtypes.float4_e2m1fn).view(np.uint8) & 0xF
        words = (c[..., 0::2] | (c[..., 1::2] << 4)).reshape(k // 512, 128, 2 * n)
    return np.ascontiguousarray(words), np.ascontiguousarray(byte.astype(np.uint8).reshape(k // 512, 16, n))


def unpack_weight(words, scales, fmt):
    g, _, n = scales.shape
    words = np.ascontiguousarray(words).reshape(g, 128, n, -1)
    if fmt == "e4m3":
        vals = words.view(ml_dtypes.float8_e4m3fn).astype(np.float64)
    else:
        nib = np.empty((g, 128, n, 4), np.uint8)
        nib[..., 0::2] = words & 0xF
        nib[..., 1::2] = words >> 4
        vals = E2M1[nib]
    vals = vals * np.repeat(np.exp2(scales.astype(np.float64) - 127.0), 8, axis=1)[..., None]
    return vals.transpose(0, 1, 3, 2).reshape(g * 512, n)


D, T, I, Q = 512, 1024, 512, 128


def setup_inputs():
    n = np.random.standard_normal
    idx = np.stack([np.random.permutation(T)[:I] for _ in range(8)])
    idx2 = np.stack([np.random.permutation(T)[:I] for _ in range(8)])
    fd = mx_kscale(D)
    keysp = pack_weight(n((D, T)) / fd[:, None], "e2m1")
    return {
        "query": (n((D, Q)) * 0.9 / np.sqrt(D) * fd[:, None]).astype(np.float32),
        "query2": (n((D, Q)) * 0.9 / np.sqrt(D) * fd[:, None]).astype(np.float32),
        "keys_words": keysp[0],
        "keys_scales": keysp[1],
        "lam": (np.random.uniform(0.5, 1.3, (Q, 1))).astype(np.float32),
        "smear": (np.random.uniform(0.3, 0.8, (Q, 1))).astype(np.float32),
        "base": (0.3 * n((Q, I))).astype(np.float32),
        "gain2": (np.random.uniform(0.5, 2.0, (Q, 1))).astype(np.float32),
        "offs": striped8(idx),
        "offs2": striped8(idx2),
    }


def reference(query, query2, keys_words, keys_scales, lam, smear, base, gain2, offs, offs2):
    idx = unstriped8(offs)
    idx2 = unstriped8(offs2)
    keysu = unpack_weight(keys_words, keys_scales, "e2m1")
    queryq = mxq(f64(query), 0, "e4m3")
    a = queryq.T @ keysu
    query2q = mxq(f64(query2), 0, "e4m3")
    b = query2q.T @ keysu
    s = (np.maximum(pick8(a, idx, 16), pick8(b, idx2, 16)) - np.maximum(pick8(a, idx2, 16), pick8(b, idx, 16))) * f64(lam)
    p = np.exp(s - np.max(s, axis=1, keepdims=True))
    r = p / np.sum(p, axis=1, keepdims=True)
    r1 = np.pad(r, ((0, 0), (1, 0)))[:, :I]
    r2 = np.pad(r, ((0, 0), (2, 0)))[:, :I]
    w = r + r1 * f64(smear) + r2 * np.square(f64(smear))
    y = np.tanh(w * f64(gain2) * 128.0) + f64(base)
    return y

@@ -1,0 +1,173 @@
+from contextlib import ExitStack
+
+import concourse.mybir as mybir
+
+D, T, I, Q = 512, 1024, 512, 128
+FLOPS = 2 * 2 * D * T * Q
+
+F32 = mybir.dt.float32
+BF16 = mybir.dt.bfloat16
+I32 = mybir.dt.int32
+U32 = mybir.dt.uint32
+U16 = mybir.dt.uint16
+U8 = mybir.dt.uint8
+FP8X4 = mybir.dt.float8_e4m3fn_x4
+FP4X4 = mybir.dt.float4_e2m1fn_x4
+ALU = mybir.AluOpType
+ACT = mybir.ActivationFunctionType
+
+P = 128
+PACK = 4
+CHUNK = 256
+HALF = I // 2
+PAD = 8
+SPANS = ((256, 256, 256, 128, 128), (256, 256, 256, 256))
+PIECES = 4
+PIECE = I // PIECES
+
+
+def tile_attend_exchanged_smeared_gated_heads_kernel(
+    tc, query, query2, keys_words, keys_scales, lam, smear, base, gain2, offs, offs2, out
+):
+    nc = tc.nc
+    with ExitStack() as ctx:
+        sb = ctx.enter_context(tc.tile_pool(name="sb", bufs=1))
+        ps = ctx.enter_context(tc.psum_pool(name="ps", bufs=1))
+
+        list1 = sb.tile([P, I // 16], U16, name="list1")
+        list2 = sb.tile([P, I // 16], U16, name="list2")
+        q_raw = [sb.tile([P, PACK, Q], F32, name="q_raw%d" % u, tag="stage%d" % u) for u in range(2)]
+        words = sb.tile([P, 2 * T], U8, name="words", align_bytes=64)
+        scales = sb.tile([P, T], U8, name="scales", align_bytes=64)
+
+        nc.vector.memset(scales[:].bitcast(I32), 0)
+        nc.sync.dma_start(out=q_raw[0][:], in_=query.rearrange("(p j) w -> p j w", j=PACK))
+        for quad in range(4):
+            nc.scalar.dma_start(
+                out=scales[32 * quad : 32 * quad + 4, :].bitcast(I32),
+                in_=keys_scales[0, 4 * quad : 4 * quad + 4, :].bitcast(I32),
+            )
+        nc.sync.dma_start(out=words[:].bitcast(I32), in_=keys_words[0].bitcast(I32))
+        nc.sync.dma_start(out=q_raw[1][:], in_=query2.rearrange("(p j) w -> p j w", j=PACK))
+        nc.sync.dma_start(list2[:], offs2)
+        nc.sync.dma_start(list1[:], offs)
+
+        score = []
+        for u in range(2):
+            grouped = sb.tile([P, Q, PACK], BF16, name="grouped%d" % u, tag="grouped%d" % u, align_bytes=64)
+            parts = 2 - u
+            width = Q // parts
+            for k in range(parts):
+                nc.vector.tensor_copy(
+                    out=grouped[:, k * width : (k + 1) * width, :],
+                    in_=q_raw[u][:, :, k * width : (k + 1) * width].rearrange("p j w -> p w j"),
+                )
+            codes = sb.tile([P, Q], U32, name="codes%d" % u, tag="codes%d" % u, align_bytes=64)
+            qsc = sb.tile([P, Q], U8, name="qsc%d" % u, align_bytes=64)
+            for k in range(parts):
+                nc.vector.quantize_mx(
+                    out=codes[:, k * width : (k + 1) * width].bitcast(FP8X4),
+                    scales=qsc[:, k * width : (k + 1) * width],
+                    in_=grouped[:, k * width : (k + 1) * width, :].rearrange("p w j -> p (w j)"),
+                )
+            full = sb.tile([P, T], F32, name="score%d" % u)
+            at = 0
+            for c, n in enumerate(SPANS[u]):
+                acc = ps.tile([P, CHUNK], F32, name="acc", tag="bank%d" % ((c + u * len(SPANS[0])) % 8))
+                nc.tensor.matmul_mx(
+                    out=acc[:, 0:n],
+                    lhsT=codes[:].bitcast(FP8X4),
+                    lhsT_scale=qsc[:],
+                    rhs=words[:, 2 * at : 2 * (at + n)].bitcast(FP4X4),
+                    rhs_scale=scales[:, at : at + n],
+                    start=True,
+                    stop=True,
+                )
+                if u == 0 and c == 3:
+                    nc.vector.tensor_copy(out=full[:, at : at + n], in_=acc[:, 0:n])
+                else:
+                    nc.scalar.activation(out=full[:, at : at + n], in_=acc[:, 0:n], func=ACT.Copy)
+                at += n
+            score.append(full)
+        a, b = score
+        base_t = sb.tile([P, I], F32, name="base_t", tag="stage0")
+        nc.sync.dma_start(out=base_t[:], in_=base)
+        gain_t = sb.tile([P, 1], F32, name="gain_t", tag="grouped0", align_bytes=64)
+        nc.sync.dma_start(out=gain_t[:], in_=gain2)
+        lam_t = sb.tile([P, 1], F32, name="lam_t", tag="stage1")
+        nc.sync.dma_start(out=lam_t[:], in_=lam)
+        smear_t = sb.tile([P, 1], F32, name="smear_t", tag="grouped1", align_bytes=64)
+        nc.sync.dma_start(out=smear_t[:], in_=smear)
+        gain128 = sb.tile([P, 1], F32, name="gain128", tag="codes1", align_bytes=64)
+        nc.scalar.activation(out=gain128[:], in_=gain_t[:], func=ACT.Copy, scale=128.0)
+        inv_gain = sb.tile([P, 1], F32, name="inv_gain")
+        nc.vector.reciprocal(inv_gain[:], gain128[:])
+
+        def cut(lst, h):
+            return lst[:, h * (HALF // 16) : (h + 1) * (HALF // 16)]
+
+        def half_tile(name):
+            return sb.tile([P, HALF], F32, name=name)
+
+        def cols(t, h):
+            return t[:, h * HALF : (h + 1) * HALF]
+
+        a2 = [half_tile("a2_%d" % h) for h in range(2)]
+        nc.vector.tensor_copy(out=a2[0][:], in_=a[:].indirect(cut(list2, 0)))
+        da1 = half_tile("da1")
+        nc.vector.tensor_tensor(da1[:], a[:].indirect(cut(list1, 0)), a2[0][:], ALU.subtract)
+        db2 = half_tile("db2")
+        nc.vector.tensor_tensor(db2[:], b[:].indirect(cut(list2, 0)), a2[0][:], ALU.subtract)
+        db1 = half_tile("db1")
+        nc.vector.tensor_tensor(db1[:], b[:].indirect(cut(list1, 0)), a2[0][:], ALU.subtract)
+        b1 = half_tile("b1")
+        nc.scalar.activation(out=b1[:], in_=b[:].indirect(cut(list1, 1)), func=ACT.Copy)
+        nc.scalar.activation(out=a2[1][:], in_=a[:].indirect(cut(list2, 1)), func=ACT.Copy)
+        a1 = half_tile("a1")
+        nc.scalar.activation(out=a1[:], in_=a[:].indirect(cut(list1, 1)), func=ACT.Copy)
+        b2 = half_tile("b2")
+        nc.scalar.activation(out=b2[:], in_=b[:].indirect(cut(list2, 1)), func=ACT.Copy)
+
+        nd = [half_tile("nd_%d" % h) for h in range(2)]
+        t = [half_tile("t_%d" % h) for h in range(2)]
+        nm = [sb.tile([P, 1], F32, name="nm_%d" % h) for h in range(2)]
+        sums = [sb.tile([P, 1], F32, name="sum_%d" % h) for h in range(2)]
+        p = sb.tile([P, PAD + I], F32, name="p")
+        nc.gpsimd.memset(p[:, 0:PAD], 0.0)
+
+        top = half_tile("top")
+        nc.vector.tensor_tensor(top[:], da1[:], db2[:], ALU.max)
+        m2 = half_tile("m2")
+        nc.vector.tensor_tensor(m2[:], a2[1][:], b1[:], ALU.max)
+        nc.vector.scalar_tensor_tensor(nd[0][:], db1[:], 0.0, top[:], ALU.max, ALU.subtract)
+        m1 = half_tile("m1")
+        nc.vector.tensor_tensor(m1[:], a1[:], b2[:], ALU.max)
+        nc.vector.tensor_scalar(t[0][:], nd[0][:], lam_t[:], None, ALU.mult, ALU.min, accum_out=nm[0][:])
+        nc.vector.tensor_tensor(nd[1][:], m2[:], m1[:], ALU.subtract)
+        nc.vector.tensor_scalar(t[1][:], nd[1][:], lam_t[:], nm[0][:], ALU.mult, ALU.min, accum_out=nm[1][:])
+
+        v = [half_tile("v%d" % h) for h in range(2)]
+        w = [half_tile("w%d" % h) for h in range(2)]
+        for h in range(2):
+            nc.scalar.activation(
+                out=p[:, PAD + h * HALF : PAD + (h + 1) * HALF], in_=t[h][:], func=ACT.Exp, bias=nm[1][:], scale=-1.0, accum_out=sums[h][:]
+            )
+
+        def back(h, k):
+            return p[:, PAD - k + h * HALF : PAD - k + (h + 1) * HALF]
+
+        for h in range(2):
+            nc.vector.scalar_tensor_tensor(v[h][:], back(h, 2), smear_t[:], back(h, 1), ALU.mult, ALU.add)
+        total = sb.tile([P, 1], F32, name="total")
+        nc.vector.tensor_scalar(total[:], sums[0][:], sums[1][:], inv_gain[:], ALU.add, ALU.mult)
+        nc.vector.scalar_tensor_tensor(w[0][:], v[0][:], smear_t[:], back(0, 0), ALU.mult, ALU.add)
+        coef = sb.tile([P, 1], F32, name="coef")
+        nc.vector.reciprocal(coef[:], total[:])
+        nc.vector.scalar_tensor_tensor(w[1][:], v[1][:], smear_t[:], back(1, 0), ALU.mult, ALU.add)
+        for c in range(PIECES):
+            h, at = divmod(c * PIECE, HALF)
+            th = sb.tile([P, PIECE], F32, name="th%d" % c)
+            nc.scalar.activation(out=th[:], in_=w[h][:, at : at + PIECE], func=ACT.Tanh, scale=coef[:])
+            y = sb.tile([P, PIECE], F32, name="y%d" % c)
+            nc.vector.tensor_tensor(y[:], th[:], base_t[:, c * PIECE : (c + 1) * PIECE], ALU.add)
+            nc.sync.dma_start(out=out[:, c * PIECE : (c + 1) * PIECE], in_=y[:])

@@ -21,6 +21,7 @@ PACK = 4
 CHUNK = 256
 HALF = I // 2
 PAD = 8
+LAST = 96
 SPANS = ((256, 256, 256, 128, 128), (256, 256, 256, 256))
 PIECES = 4
 PIECE = I // PIECES
@@ -37,18 +38,19 @@ def tile_attend_exchanged_smeared_gated_heads_kernel(
         list1 = sb.tile([P, I // 16], U16, name="list1")
         list2 = sb.tile([P, I // 16], U16, name="list2")
         q_raw = [sb.tile([P, PACK, Q], F32, name="q_raw%d" % u, tag="stage%d" % u) for u in range(2)]
-        words = sb.tile([P, 2 * T], U8, name="words", align_bytes=64)
+        words = [sb.tile([P, T], U8, name="words%d" % k, align_bytes=64) for k in range(2)]
         scales = sb.tile([P, T], U8, name="scales", align_bytes=64)
 
-        nc.vector.memset(scales[:].bitcast(I32), 0)
+        nc.gpsimd.memset(scales[:].bitcast(I32), 0)
         nc.sync.dma_start(out=q_raw[0][:], in_=query.rearrange("(p j) w -> p j w", j=PACK))
         for quad in range(4):
             nc.scalar.dma_start(
                 out=scales[32 * quad : 32 * quad + 4, :].bitcast(I32),
                 in_=keys_scales[0, 4 * quad : 4 * quad + 4, :].bitcast(I32),
             )
-        nc.sync.dma_start(out=words[:].bitcast(I32), in_=keys_words[0].bitcast(I32))
+        nc.sync.dma_start(out=words[0][:].bitcast(I32), in_=keys_words[0, :, 0:T].bitcast(I32))
         nc.sync.dma_start(out=q_raw[1][:], in_=query2.rearrange("(p j) w -> p j w", j=PACK))
+        nc.sync.dma_start(out=words[1][:].bitcast(I32), in_=keys_words[0, :, T : 2 * T].bitcast(I32))
         nc.sync.dma_start(list2[:], offs2)
         nc.sync.dma_start(list1[:], offs)
 
@@ -78,7 +80,7 @@ def tile_attend_exchanged_smeared_gated_heads_kernel(
                     out=acc[:, 0:n],
                     lhsT=codes[:].bitcast(FP8X4),
                     lhsT_scale=qsc[:],
-                    rhs=words[:, 2 * at : 2 * (at + n)].bitcast(FP4X4),
+                    rhs=words[2 * at // T][:, 2 * at % T : 2 * at % T + 2 * n].bitcast(FP4X4),
                     rhs_scale=scales[:, at : at + n],
                     start=True,
                     stop=True,
@@ -98,10 +100,6 @@ def tile_attend_exchanged_smeared_gated_heads_kernel(
         nc.sync.dma_start(out=lam_t[:], in_=lam)
         smear_t = sb.tile([P, 1], F32, name="smear_t", tag="grouped1", align_bytes=64)
         nc.sync.dma_start(out=smear_t[:], in_=smear)
-        gain128 = sb.tile([P, 1], F32, name="gain128", tag="codes1", align_bytes=64)
-        nc.scalar.activation(out=gain128[:], in_=gain_t[:], func=ACT.Copy, scale=128.0)
-        inv_gain = sb.tile([P, 1], F32, name="inv_gain")
-        nc.vector.reciprocal(inv_gain[:], gain128[:])
 
         def cut(lst, h):
             return lst[:, h * (HALF // 16) : (h + 1) * (HALF // 16)]
@@ -120,20 +118,20 @@ def tile_attend_exchanged_smeared_gated_heads_kernel(
         nc.vector.tensor_tensor(db2[:], b[:].indirect(cut(list2, 0)), a2[0][:], ALU.subtract)
         db1 = half_tile("db1")
         nc.vector.tensor_tensor(db1[:], b[:].indirect(cut(list1, 0)), a2[0][:], ALU.subtract)
-        b1 = half_tile("b1")
-        nc.scalar.activation(out=b1[:], in_=b[:].indirect(cut(list1, 1)), func=ACT.Copy)
         nc.scalar.activation(out=a2[1][:], in_=a[:].indirect(cut(list2, 1)), func=ACT.Copy)
+        b1 = sb.tile([P, HALF], F32, name="b1", tag="b1")
+        nc.scalar.activation(out=b1[:], in_=b[:].indirect(cut(list1, 1)), func=ACT.Copy)
         a1 = half_tile("a1")
         nc.scalar.activation(out=a1[:], in_=a[:].indirect(cut(list1, 1)), func=ACT.Copy)
         b2 = half_tile("b2")
         nc.scalar.activation(out=b2[:], in_=b[:].indirect(cut(list2, 1)), func=ACT.Copy)
 
         nd = [half_tile("nd_%d" % h) for h in range(2)]
-        t = [half_tile("t_%d" % h) for h in range(2)]
+        t = sb.tile([P, I], F32, name="t")
         nm = [sb.tile([P, 1], F32, name="nm_%d" % h) for h in range(2)]
         sums = [sb.tile([P, 1], F32, name="sum_%d" % h) for h in range(2)]
-        p = sb.tile([P, PAD + I], F32, name="p")
-        nc.gpsimd.memset(p[:, 0:PAD], 0.0)
+        p = [sb.tile([P, PAD + HALF], F32, name="p_%d" % h) for h in range(2)]
+        nc.gpsimd.memset(p[0][:, 0:PAD], 0.0)
 
         top = half_tile("top")
         nc.vector.tensor_tensor(top[:], da1[:], db2[:], ALU.max)
@@ -142,32 +140,53 @@ def tile_attend_exchanged_smeared_gated_heads_kernel(
         nc.vector.scalar_tensor_tensor(nd[0][:], db1[:], 0.0, top[:], ALU.max, ALU.subtract)
         m1 = half_tile("m1")
         nc.vector.tensor_tensor(m1[:], a1[:], b2[:], ALU.max)
-        nc.vector.tensor_scalar(t[0][:], nd[0][:], lam_t[:], None, ALU.mult, ALU.min, accum_out=nm[0][:])
+        nc.vector.tensor_scalar(cols(t, 0), nd[0][:], lam_t[:], None, ALU.mult, ALU.min, accum_out=nm[0][:])
         nc.vector.tensor_tensor(nd[1][:], m2[:], m1[:], ALU.subtract)
-        nc.vector.tensor_scalar(t[1][:], nd[1][:], lam_t[:], nm[0][:], ALU.mult, ALU.min, accum_out=nm[1][:])
+        nc.vector.tensor_scalar(cols(t, 1), nd[1][:], lam_t[:], nm[0][:], ALU.mult, ALU.min, accum_out=nm[1][:])
+
+        gain128 = sb.tile([P, 1], F32, name="gain128", tag="b1")
+        nc.scalar.activation(out=gain128[:], in_=gain_t[:], func=ACT.Copy, scale=128.0)
+        inv_gain = sb.tile([P, 1], F32, name="inv_gain")
+        nc.vector.reciprocal(inv_gain[:], gain128[:])
+
+        edge = HALF - 2
+        nc.scalar.activation(
+            out=p[0][:, PAD : PAD + edge], in_=t[:, 0:edge], func=ACT.Exp, bias=nm[0][:], scale=-1.0, accum_out=sums[0][:]
+        )
+        nc.scalar.activation(out=p[0][:, PAD + edge :], in_=t[:, edge:HALF], func=ACT.Exp, bias=nm[0][:], scale=-1.0)
+        shrink = sb.tile([P, 1], F32, name="shrink")
+        nc.scalar.activation(out=shrink[:], in_=nm[0][:], func=ACT.Exp, bias=nm[1][:], scale=-1.0)
+        nc.scalar.activation(
+            out=p[1][:, PAD - 2 :], in_=t[:, edge:], func=ACT.Exp, bias=nm[1][:], scale=-1.0, accum_out=sums[1][:]
+        )
+        sum0s = sb.tile([P, 1], F32, name="sum0s")
+        nc.scalar.activation(out=sum0s[:], in_=shrink[:], func=ACT.Copy, scale=sums[0][:])
 
         v = [half_tile("v%d" % h) for h in range(2)]
         w = [half_tile("w%d" % h) for h in range(2)]
-        for h in range(2):
-            nc.scalar.activation(
-                out=p[:, PAD + h * HALF : PAD + (h + 1) * HALF], in_=t[h][:], func=ACT.Exp, bias=nm[1][:], scale=-1.0, accum_out=sums[h][:]
+
+        def near(h, lo, hi):
+            nc.vector.scalar_tensor_tensor(
+                v[h][:, lo:hi], p[h][:, PAD - 2 + lo : PAD - 2 + hi], smear_t[:], p[h][:, PAD - 1 + lo : PAD - 1 + hi], ALU.mult, ALU.add
             )
 
-        def back(h, k):
-            return p[:, PAD - k + h * HALF : PAD - k + (h + 1) * HALF]
+        def weight(h, lo, hi):
+            nc.vector.scalar_tensor_tensor(w[h][:, lo:hi], v[h][:, lo:hi], smear_t[:], p[h][:, PAD + lo : PAD + hi], ALU.mult, ALU.add)
 
-        for h in range(2):
-            nc.vector.scalar_tensor_tensor(v[h][:], back(h, 2), smear_t[:], back(h, 1), ALU.mult, ALU.add)
+        near(0, 0, HALF)
+        weight(0, 0, HALF)
+        near(1, 0, PIECE)
         total = sb.tile([P, 1], F32, name="total")
-        nc.vector.tensor_scalar(total[:], sums[0][:], sums[1][:], inv_gain[:], ALU.add, ALU.mult)
-        nc.vector.scalar_tensor_tensor(w[0][:], v[0][:], smear_t[:], back(0, 0), ALU.mult, ALU.add)
-        coef = sb.tile([P, 1], F32, name="coef")
-        nc.vector.reciprocal(coef[:], total[:])
-        nc.vector.scalar_tensor_tensor(w[1][:], v[1][:], smear_t[:], back(1, 0), ALU.mult, ALU.add)
-        for c in range(PIECES):
-            h, at = divmod(c * PIECE, HALF)
-            th = sb.tile([P, PIECE], F32, name="th%d" % c)
-            nc.scalar.activation(out=th[:], in_=w[h][:, at : at + PIECE], func=ACT.Tanh, scale=coef[:])
-            y = sb.tile([P, PIECE], F32, name="y%d" % c)
-            nc.vector.tensor_tensor(y[:], th[:], base_t[:, c * PIECE : (c + 1) * PIECE], ALU.add)
-            nc.sync.dma_start(out=out[:, c * PIECE : (c + 1) * PIECE], in_=y[:])
+        nc.vector.tensor_scalar(total[:], sums[1][:], sum0s[:], inv_gain[:], ALU.add, ALU.mult)
+        near(1, PIECE, HALF)
+        coef = [sb.tile([P, 1], F32, name="coef%d" % h) for h in range(2)]
+        nc.vector.reciprocal(coef[1][:], total[:])
+        weight(1, 0, PIECE)
+        weight(1, PIECE, HALF)
+        nc.scalar.activation(out=coef[0][:], in_=coef[1][:], func=ACT.Copy, scale=shrink[:])
+        for c, (h, lo, hi) in enumerate(((1, 0, PIECE), (1, PIECE, HALF), (0, 0, HALF - LAST), (0, HALF - LAST, HALF))):
+            th = sb.tile([P, hi - lo], F32, name="th%d" % c)
+            nc.scalar.activation(out=th[:], in_=w[h][:, lo:hi], func=ACT.Tanh, scale=coef[h][:])
+            y = sb.tile([P, hi - lo], F32, name="y%d" % c)
+            nc.vector.tensor_tensor(y[:], th[:], base_t[:, h * HALF + lo : h * HALF + hi], ALU.add)
+            nc.sync.dma_start(out=out[:, h * HALF + lo : h * HALF + hi], in_=y[:])

@@ -22,7 +22,8 @@ CHUNK = 256
 HALF = I // 2
 PAD = 8
 LAST = 96
-SPANS = ((256, 256, 256, 128, 128), (256, 256, 256, 256))
+SPANS = ((256, 256, 256, 128, 128), (256, 256, 256, 128, 128))
+BANKS = ((0, 1, 2, 3, 4), (5, 6, 7, 0, 4))
 PIECES = 4
 PIECE = I // PIECES
 
@@ -75,7 +76,7 @@ def tile_attend_exchanged_smeared_gated_heads_kernel(
             full = sb.tile([P, T], F32, name="score%d" % u)
             at = 0
             for c, n in enumerate(SPANS[u]):
-                acc = ps.tile([P, CHUNK], F32, name="acc", tag="bank%d" % ((c + u * len(SPANS[0])) % 8))
+                acc = ps.tile([P, CHUNK], F32, name="acc", tag="bank%d" % BANKS[u][c])
                 nc.tensor.matmul_mx(
                     out=acc[:, 0:n],
                     lhsT=codes[:].bitcast(FP8X4),
@@ -85,7 +86,7 @@ def tile_attend_exchanged_smeared_gated_heads_kernel(
                     start=True,
                     stop=True,
                 )
-                if u == 0 and c == 3:
+                if c == 3 + u:
                     nc.vector.tensor_copy(out=full[:, at : at + n], in_=acc[:, 0:n])
                 else:
                     nc.scalar.activation(out=full[:, at : at + n], in_=acc[:, 0:n], func=ACT.Copy)
@@ -183,10 +184,11 @@ def tile_attend_exchanged_smeared_gated_heads_kernel(
         nc.vector.reciprocal(coef[1][:], total[:])
         weight(1, 0, PIECE)
         weight(1, PIECE, HALF)
-        nc.scalar.activation(out=coef[0][:], in_=coef[1][:], func=ACT.Copy, scale=shrink[:])
+        nc.vector.tensor_scalar(coef[0][:], coef[1][:], shrink[:], None, ALU.mult)
         for c, (h, lo, hi) in enumerate(((1, 0, PIECE), (1, PIECE, HALF), (0, 0, HALF - LAST), (0, HALF - LAST, HALF))):
             th = sb.tile([P, hi - lo], F32, name="th%d" % c)
             nc.scalar.activation(out=th[:], in_=w[h][:, lo:hi], func=ACT.Tanh, scale=coef[h][:])
             y = sb.tile([P, hi - lo], F32, name="y%d" % c)
             nc.vector.tensor_tensor(y[:], th[:], base_t[:, h * HALF + lo : h * HALF + hi], ALU.add)
-            nc.sync.dma_start(out=out[:, h * HALF + lo : h * HALF + hi], in_=y[:])
+            queue = nc.scalar if c == 3 else nc.sync
+            queue.dma_start(out=out[:, h * HALF + lo : h * HALF + hi], in_=y[:])

@@ -190,5 +190,4 @@ def tile_attend_exchanged_smeared_gated_heads_kernel(
             nc.scalar.activation(out=th[:], in_=w[h][:, lo:hi], func=ACT.Tanh, scale=coef[h][:])
             y = sb.tile([P, hi - lo], F32, name="y%d" % c)
             nc.vector.tensor_tensor(y[:], th[:], base_t[:, h * HALF + lo : h * HALF + hi], ALU.add)
-            queue = nc.scalar if c == 3 else nc.sync
-            queue.dma_start(out=out[:, h * HALF + lo : h * HALF + hi], in_=y[:])
+            nc.sync.dma_start(out=out[:, h * HALF + lo : h * HALF + hi], in_=y[:])

from contextlib import ExitStack

import concourse.mybir as mybir

D, T, I, Q = 512, 1024, 512, 128
FLOPS = 2 * 2 * D * T * Q

F32 = mybir.dt.float32
BF16 = mybir.dt.bfloat16
I32 = mybir.dt.int32
U32 = mybir.dt.uint32
U16 = mybir.dt.uint16
U8 = mybir.dt.uint8
FP8X4 = mybir.dt.float8_e4m3fn_x4
FP4X4 = mybir.dt.float4_e2m1fn_x4
ALU = mybir.AluOpType
ACT = mybir.ActivationFunctionType

P = 128
PACK = 4
CHUNK = 256
HALF = I // 2
PAD = 8
LAST = 96
SPANS = ((256, 256, 256, 128, 128), (256, 256, 256, 128, 128))
BANKS = ((0, 1, 2, 3, 4), (5, 6, 7, 0, 4))
PIECES = 4
PIECE = I // PIECES


def tile_attend_exchanged_smeared_gated_heads_kernel(
    tc, query, query2, keys_words, keys_scales, lam, smear, base, gain2, offs, offs2, out
):
    nc = tc.nc
    with ExitStack() as ctx:
        sb = ctx.enter_context(tc.tile_pool(name="sb", bufs=1))
        ps = ctx.enter_context(tc.psum_pool(name="ps", bufs=1))

        list1 = sb.tile([P, I // 16], U16, name="list1")
        list2 = sb.tile([P, I // 16], U16, name="list2")
        q_raw = [sb.tile([P, PACK, Q], F32, name="q_raw%d" % u, tag="stage%d" % u) for u in range(2)]
        words = [sb.tile([P, T], U8, name="words%d" % k, align_bytes=64) for k in range(2)]
        scales = sb.tile([P, T], U8, name="scales", align_bytes=64)

        nc.gpsimd.memset(scales[:].bitcast(I32), 0)
        nc.sync.dma_start(out=q_raw[0][:], in_=query.rearrange("(p j) w -> p j w", j=PACK))
        for quad in range(4):
            nc.scalar.dma_start(
                out=scales[32 * quad : 32 * quad + 4, :].bitcast(I32),
                in_=keys_scales[0, 4 * quad : 4 * quad + 4, :].bitcast(I32),
            )
        nc.sync.dma_start(out=words[0][:].bitcast(I32), in_=keys_words[0, :, 0:T].bitcast(I32))
        nc.sync.dma_start(out=q_raw[1][:], in_=query2.rearrange("(p j) w -> p j w", j=PACK))
        nc.sync.dma_start(out=words[1][:].bitcast(I32), in_=keys_words[0, :, T : 2 * T].bitcast(I32))
        nc.sync.dma_start(list2[:], offs2)
        nc.sync.dma_start(list1[:], offs)

        score = []
        for u in range(2):
            grouped = sb.tile([P, Q, PACK], BF16, name="grouped%d" % u, tag="grouped%d" % u, align_bytes=64)
            parts = 2 - u
            width = Q // parts
            for k in range(parts):
                nc.vector.tensor_copy(
                    out=grouped[:, k * width : (k + 1) * width, :],
                    in_=q_raw[u][:, :, k * width : (k + 1) * width].rearrange("p j w -> p w j"),
                )
            codes = sb.tile([P, Q], U32, name="codes%d" % u, tag="codes%d" % u, align_bytes=64)
            qsc = sb.tile([P, Q], U8, name="qsc%d" % u, align_bytes=64)
            for k in range(parts):
                nc.vector.quantize_mx(
                    out=codes[:, k * width : (k + 1) * width].bitcast(FP8X4),
                    scales=qsc[:, k * width : (k + 1) * width],
                    in_=grouped[:, k * width : (k + 1) * width, :].rearrange("p w j -> p (w j)"),
                )
            full = sb.tile([P, T], F32, name="score%d" % u)
            at = 0
            for c, n in enumerate(SPANS[u]):
                acc = ps.tile([P, CHUNK], F32, name="acc", tag="bank%d" % BANKS[u][c])
                nc.tensor.matmul_mx(
                    out=acc[:, 0:n],
                    lhsT=codes[:].bitcast(FP8X4),
                    lhsT_scale=qsc[:],
                    rhs=words[2 * at // T][:, 2 * at % T : 2 * at % T + 2 * n].bitcast(FP4X4),
                    rhs_scale=scales[:, at : at + n],
                    start=True,
                    stop=True,
                )
                if c == 3 + u:
                    nc.vector.tensor_copy(out=full[:, at : at + n], in_=acc[:, 0:n])
                else:
                    nc.scalar.activation(out=full[:, at : at + n], in_=acc[:, 0:n], func=ACT.Copy)
                at += n
            score.append(full)
        a, b = score
        base_t = sb.tile([P, I], F32, name="base_t", tag="stage0")
        nc.sync.dma_start(out=base_t[:], in_=base)
        gain_t = sb.tile([P, 1], F32, name="gain_t", tag="grouped0", align_bytes=64)
        nc.sync.dma_start(out=gain_t[:], in_=gain2)
        lam_t = sb.tile([P, 1], F32, name="lam_t", tag="stage1")
        nc.sync.dma_start(out=lam_t[:], in_=lam)
        smear_t = sb.tile([P, 1], F32, name="smear_t", tag="grouped1", align_bytes=64)
        nc.sync.dma_start(out=smear_t[:], in_=smear)

        def cut(lst, h):
            return lst[:, h * (HALF // 16) : (h + 1) * (HALF // 16)]

        def half_tile(name):
            return sb.tile([P, HALF], F32, name=name)

        def cols(t, h):
            return t[:, h * HALF : (h + 1) * HALF]

        a2 = [half_tile("a2_%d" % h) for h in range(2)]
        nc.vector.tensor_copy(out=a2[0][:], in_=a[:].indirect(cut(list2, 0)))
        da1 = half_tile("da1")
        nc.vector.tensor_tensor(da1[:], a[:].indirect(cut(list1, 0)), a2[0][:], ALU.subtract)
        db2 = half_tile("db2")
        nc.vector.tensor_tensor(db2[:], b[:].indirect(cut(list2, 0)), a2[0][:], ALU.subtract)
        db1 = half_tile("db1")
        nc.vector.tensor_tensor(db1[:], b[:].indirect(cut(list1, 0)), a2[0][:], ALU.subtract)
        nc.scalar.activation(out=a2[1][:], in_=a[:].indirect(cut(list2, 1)), func=ACT.Copy)
        b1 = sb.tile([P, HALF], F32, name="b1", tag="b1")
        nc.scalar.activation(out=b1[:], in_=b[:].indirect(cut(list1, 1)), func=ACT.Copy)
        a1 = half_tile("a1")
        nc.scalar.activation(out=a1[:], in_=a[:].indirect(cut(list1, 1)), func=ACT.Copy)
        b2 = half_tile("b2")
        nc.scalar.activation(out=b2[:], in_=b[:].indirect(cut(list2, 1)), func=ACT.Copy)

        nd = [half_tile("nd_%d" % h) for h in range(2)]
        t = sb.tile([P, I], F32, name="t")
        nm = [sb.tile([P, 1], F32, name="nm_%d" % h) for h in range(2)]
        sums = [sb.tile([P, 1], F32, name="sum_%d" % h) for h in range(2)]
        p = [sb.tile([P, PAD + HALF], F32, name="p_%d" % h) for h in range(2)]
        nc.gpsimd.memset(p[0][:, 0:PAD], 0.0)

        top = half_tile("top")
        nc.vector.tensor_tensor(top[:], da1[:], db2[:], ALU.max)
        m2 = half_tile("m2")
        nc.vector.tensor_tensor(m2[:], a2[1][:], b1[:], ALU.max)
        nc.vector.scalar_tensor_tensor(nd[0][:], db1[:], 0.0, top[:], ALU.max, ALU.subtract)
        m1 = half_tile("m1")
        nc.vector.tensor_tensor(m1[:], a1[:], b2[:], ALU.max)
        nc.vector.tensor_scalar(cols(t, 0), nd[0][:], lam_t[:], None, ALU.mult, ALU.min, accum_out=nm[0][:])
        nc.vector.tensor_tensor(nd[1][:], m2[:], m1[:], ALU.subtract)
        nc.vector.tensor_scalar(cols(t, 1), nd[1][:], lam_t[:], nm[0][:], ALU.mult, ALU.min, accum_out=nm[1][:])

        gain128 = sb.tile([P, 1], F32, name="gain128", tag="b1")
        nc.scalar.activation(out=gain128[:], in_=gain_t[:], func=ACT.Copy, scale=128.0)
        inv_gain = sb.tile([P, 1], F32, name="inv_gain")
        nc.vector.reciprocal(inv_gain[:], gain128[:])

        edge = HALF - 2
        nc.scalar.activation(
            out=p[0][:, PAD : PAD + edge], in_=t[:, 0:edge], func=ACT.Exp, bias=nm[0][:], scale=-1.0, accum_out=sums[0][:]
        )
        nc.scalar.activation(out=p[0][:, PAD + edge :], in_=t[:, edge:HALF], func=ACT.Exp, bias=nm[0][:], scale=-1.0)
        shrink = sb.tile([P, 1], F32, name="shrink")
        nc.scalar.activation(out=shrink[:], in_=nm[0][:], func=ACT.Exp, bias=nm[1][:], scale=-1.0)
        nc.scalar.activation(
            out=p[1][:, PAD - 2 :], in_=t[:, edge:], func=ACT.Exp, bias=nm[1][:], scale=-1.0, accum_out=sums[1][:]
        )
        sum0s = sb.tile([P, 1], F32, name="sum0s")
        nc.scalar.activation(out=sum0s[:], in_=shrink[:], func=ACT.Copy, scale=sums[0][:])

        v = [half_tile("v%d" % h) for h in range(2)]
        w = [half_tile("w%d" % h) for h in range(2)]

        def near(h, lo, hi):
            nc.vector.scalar_tensor_tensor(
                v[h][:, lo:hi], p[h][:, PAD - 2 + lo : PAD - 2 + hi], smear_t[:], p[h][:, PAD - 1 + lo : PAD - 1 + hi], ALU.mult, ALU.add
            )

        def weight(h, lo, hi):
            nc.vector.scalar_tensor_tensor(w[h][:, lo:hi], v[h][:, lo:hi], smear_t[:], p[h][:, PAD + lo : PAD + hi], ALU.mult, ALU.add)

        near(0, 0, HALF)
        weight(0, 0, HALF)
        near(1, 0, PIECE)
        total = sb.tile([P, 1], F32, name="total")
        nc.vector.tensor_scalar(total[:], sums[1][:], sum0s[:], inv_gain[:], ALU.add, ALU.mult)
        near(1, PIECE, HALF)
        coef = [sb.tile([P, 1], F32, name="coef%d" % h) for h in range(2)]
        nc.vector.reciprocal(coef[1][:], total[:])
        weight(1, 0, PIECE)
        weight(1, PIECE, HALF)
        nc.vector.tensor_scalar(coef[0][:], coef[1][:], shrink[:], None, ALU.mult)
        for c, (h, lo, hi) in enumerate(((1, 0, PIECE), (1, PIECE, HALF), (0, 0, HALF - LAST), (0, HALF - LAST, HALF))):
            th = sb.tile([P, hi - lo], F32, name="th%d" % c)
            nc.scalar.activation(out=th[:], in_=w[h][:, lo:hi], func=ACT.Tanh, scale=coef[h][:])
            y = sb.tile([P, hi - lo], F32, name="y%d" % c)
            nc.vector.tensor_tensor(y[:], th[:], base_t[:, h * HALF + lo : h * HALF + hi], ALU.add)
            nc.sync.dma_start(out=out[:, h * HALF + lo : h * HALF + hi], in_=y[:])
